import numpy as np
import ml_dtypes


def mxq(x, axis, fmt="e4m3"):
    dtype, down = {"e4m3": (ml_dtypes.float8_e4m3fn, 7), "e5m2": (ml_dtypes.float8_e5m2, 14)}[fmt]
    v = np.moveaxis(np.asarray(x, np.float32).astype(ml_dtypes.bfloat16).astype(np.float64), axis, -1)
    blocks = v.reshape(v.shape[:-1] + (-1, 32))
    amax = np.abs(blocks).max(-1, keepdims=True)
    byte = np.maximum(np.where(amax > 0, np.frexp(amax)[1] - 1 + 127, 0) - down, 1)
    scale = np.exp2(byte - 127.0)
    codes = (blocks / scale).astype(np.float32).astype(dtype).astype(np.float64)
    return np.moveaxis((codes * scale).reshape(v.shape), -1, axis)


WIDE = False


def mx_kscale(k):
    if not WIDE:
        return np.ones(k)
    levels = np.array([24, -24, 12, -12, 0])
    if k % 512:
        return np.exp2(np.random.permutation(np.resize(levels, k // 32))).repeat(32)
    a = np.empty((k // 512, 16))
    for p in range(k // 512):
        a[p, :8] = np.random.permutation(np.resize(levels, 8))
        for g in range(8):
            far = levels[np.abs(levels - a[p, g]) >= 10]
            a[p, g + 8] = far[np.random.randint(len(far))]
    return np.exp2(a.ravel()).repeat(32)


def f64(x):
    return np.asarray(x).astype(np.float64)


E2M1 = np.array([0.0, 0.5, 1.0, 1.5, 2.0, 3.0, 4.0, 6.0, -0.0, -0.5, -1.0, -1.5, -2.0, -3.0, -4.0, -6.0])


def pack_weight(w, fmt):
    k, n = w.shape
    w = f64(np.asarray(w, np.float32).astype(ml_dtypes.bfloat16)).reshape(k // 32, 32, n)
    amax = np.abs(w).max(1)
    if fmt == "e4m3":
        byte = np.frexp(amax)[1] - 1 + 127 - 7
    else:
        mant, ex = np.frexp(amax / 6.0)
        byte = np.where(mant > 0.5, ex, ex - 1) + 127
    byte = np.clip(np.where(amax > 0, byte, 1), 1, 254)
    scaled = (w * np.exp2(127.0 - byte)[:, None, :]).reshape(k, n).astype(np.float32)
    by_word = np.ascontiguousarray(scaled.reshape(k // 512, 128, 4, n).transpose(0, 1, 3, 2))
    if fmt == "e4m3":
        words = by_word.astype(ml_dtypes.float8_e4m3fn).view(np.uint8)
    else:
        c = by_word.astype(ml_dtypes.float4_e2m1fn).view(np.uint8) & 0xF
        words = (c[..., 0::2] | (c[..., 1::2] << 4)).reshape(k // 512, 128, 2 * n)
    return np.ascontiguousarray(words), np.ascontiguousarray(byte.astype(np.uint8).reshape(k // 512, 16, n))


def unpack_weight(words, scales, fmt):
    g, _, n = scales.shape
    words = np.ascontiguousarray(words).reshape(g, 128, n, -1)
    if fmt == "e4m3":
        vals = words.view(ml_dtypes.float8_e4m3fn).astype(np.float64)
    else:
        nib = np.empty((g, 128, n, 4), np.uint8)
        nib[..., 0::2] = words & 0xF
        nib[..., 1::2] = words >> 4
        vals = E2M1[nib]
    vals = vals * np.repeat(np.exp2(scales.astype(np.float64) - 127.0), 8, axis=1)[..., None]
    return vals.transpose(0, 1, 3, 2).reshape(g * 512, n)


def planes(y):
    n, m = y.shape
    v = y.astype(np.float32).astype(ml_dtypes.bfloat16).astype(np.float64).reshape(n // 32, 32, m)
    top = np.abs(v).max(1)
    byte = np.clip(np.where(top > 0, np.frexp(top)[1] - 1 + 127 - 7, 1), 1, 254)
    codes = (v * np.exp2(127.0 - byte)[:, None, :]).reshape(n, m).astype(np.float32).astype(ml_dtypes.float8_e4m3fn).view(np.uint8)
    words = codes.reshape(n // 512, 128, 4, m).transpose(0, 1, 3, 2)
    return np.ascontiguousarray(words), np.ascontiguousarray(byte.astype(np.uint8).reshape(n // 512, 16, m))


K, D, M, J = 1024, 512, 1024, 1024


def setup_inputs():
    n = np.random.standard_normal
    u = mx_kscale(D)[:, None]
    s3 = mx_kscale(K)[:, None]
    s = mx_kscale(K)[:, None]
    p_w4 = pack_weight(n((K, D)) / np.sqrt(K) / s / u.T, "e2m1")
    return {
        "x": (n((K, M)) * s).astype(np.float32),
        "w4_words": p_w4[0],
        "w4_scales": p_w4[1],
        "c": (n((K, J)) * s3).astype(np.float32),
        "wk": (n((K, D)) / np.sqrt(K) / s3 * u.T).astype(np.float32),
        "kb": (0.3 * n(J)).astype(np.float32),
    }


def reference(x, w4_words, w4_scales, c, wk, kb):
    x_ = mxq(f64(x), 0, "e4m3")
    w4_ = unpack_weight(w4_words, w4_scales, "e2m1")
    qr = w4_.T @ x_
    qr_ = mxq(qr, 0, "e4m3")
    c_ = mxq(f64(c), 0, "e4m3")
    wk_ = mxq(f64(wk), 0, "e4m3")
    kc = wk_.T @ c_
    kc_ = mxq(kc, 0, "e4m3")
    sc = qr_.T @ kc_
    return (sc * 0.03125 + f64(kb)[None, :], kc) + planes(kc)

@@ -1,0 +1,311 @@
+from contextlib import ExitStack
+
+import concourse.mybir as mybir
+from concourse.masks import make_identity
+
+K, D, M, J = 1024, 512, 1024, 1024
+FLOPS = 2 * K * D * M + 2 * K * D * J + 2 * D * M * J
+
+F32 = mybir.dt.float32
+BF16 = mybir.dt.bfloat16
+I32 = mybir.dt.int32
+U32 = mybir.dt.uint32
+U8 = mybir.dt.uint8
+FP8X4 = mybir.dt.float8_e4m3fn_x4
+FP4X4 = mybir.dt.float4_e2m1fn_x4
+ALU = mybir.AluOpType
+
+P = 128
+PACK = 4
+K_PASS = P * PACK
+HALF = 512
+GROUPS = HALF // PACK
+SCORE_SCALE = 0.03125
+C_SPLIT = 84
+X_SPLIT = 64
+
+
+def tile_mix_kvw_bias_kernel(tc, x, w4_words, w4_scales, c, wk, kb, out_0, out_1, out_2, out_3):
+    nc = tc.nc
+    with ExitStack() as ctx:
+        keep = ctx.enter_context(tc.tile_pool(name="keep", bufs=1))
+        stage = ctx.enter_context(tc.tile_pool(name="stage", bufs=6))
+        small = ctx.enter_context(tc.tile_pool(name="small", bufs=4))
+        psum = ctx.enter_context(tc.psum_pool(name="psum", bufs=1))
+        ctx.enter_context(tc.manual_schedule())
+
+        def bank(b, name):
+            return psum.tile([P, HALF], F32, tag="bank%d" % b, name=name)
+
+        def load_rows(name, src, a, cols):
+            width = cols.stop - cols.start
+            raw = keep.tile([P, PACK, width], F32, name=name)
+            nc.sync.dma_start(out=raw[:], in_=src[a * K_PASS : (a + 1) * K_PASS, cols].rearrange("(p t) w -> p t w", t=PACK))
+            return raw
+
+        def mx_tiles(name, width):
+            codes = keep.tile([P, width], U32, name=name + "_codes", align_bytes=64)
+            scales = keep.tile([P, width], U8, name=name + "_scales", align_bytes=64)
+            return codes, scales
+
+        def staged(name):
+            return stage.tile([P, HALF * PACK], BF16, tag="staged", name=name, align_bytes=64)
+
+        def copy_on(engine, dst, src):
+            if engine == "vector":
+                nc.vector.tensor_copy(out=dst, in_=src)
+            else:
+                nc.scalar.copy(out=dst, in_=src)
+
+        def interleave(engine, dst, rows, g0, g1):
+            copy_on(
+                engine,
+                dst[:].rearrange("p (g i t) -> p g t i", i=PACK, t=PACK)[:, g0:g1],
+                rows.rearrange("p t (g i) -> p g t i", i=PACK)[:, g0:g1],
+            )
+
+        def interleave_dealt(engine, dst, rows, g0, g1):
+            copy_on(
+                engine,
+                dst[:].rearrange("p (u g t) -> p g t u", u=PACK, t=PACK)[:, g0:g1],
+                rows.rearrange("p t (g u) -> p g t u", u=PACK)[:, g0:g1],
+            )
+
+        def quantize(src, codes, scales):
+            nc.vector.quantize_mx(out=codes.bitcast(FP8X4), scales=scales, in_=src)
+
+        w4_raw = keep.tile([P, 2, 2 * D], U8, name="w4_raw")
+        nc.sync.dma_start(out=w4_raw[:], in_=w4_words.rearrange("a p n -> p a n"))
+        c_raw = [None, None]
+        wk_raw = [None, None]
+        w4s_raw = keep.tile([P, 2, D], U8, name="w4s_raw")
+        nc.vector.memset(w4s_raw[:].bitcast(I32), 0)
+        for q in range(4):
+            nc.sync.dma_start(
+                out=w4s_raw[32 * q : 32 * q + 4].bitcast(I32),
+                in_=w4_scales[:, 4 * q : 4 * q + 4, :].rearrange("a r n -> r a n").bitcast(I32),
+            )
+        kb_cols = keep.tile([P, J // P], F32, name="kb_cols")
+        nc.sync.dma_start(out=kb_cols[:], in_=kb.rearrange("(p e) -> p e", e=J // P))
+        c_raw[0] = load_rows("c_raw0", c, 0, slice(0, J))
+        wk_raw[0] = load_rows("wk_raw0", wk, 0, slice(0, D))
+        wk_raw[1] = load_rows("wk_raw1", wk, 1, slice(0, D))
+        c1_raw = [load_rows("c_raw1_%d" % h, c, 1, slice(h * HALF, (h + 1) * HALF)) for h in range(2)]
+        x0_raw = load_rows("x_raw0", x, 0, slice(0, M))
+        x1_raw = [load_rows("x_raw1_%d" % h, x, 1, slice(h * HALF, (h + 1) * HALF)) for h in range(2)]
+
+        ident = keep.tile([P, P], F32, name="ident")
+        make_identity(nc, ident[:])
+
+        w4_codes = keep.tile([P, 2, PACK, 2 * P], U8, name="w4_codes", align_bytes=64)
+        w4_sc = keep.tile([P, 2, PACK, P], U8, name="w4_sc", align_bytes=64)
+        for a in range(2):
+            nc.vector.tensor_copy(
+                out=w4_codes[:, a].rearrange("p u (g b) -> p g u b", b=2),
+                in_=w4_raw[:, a].rearrange("p (g u b) -> p g u b", u=PACK, b=2),
+            )
+
+        nc.vector.tensor_copy(
+            out=w4_sc[:].rearrange("p a u g -> p a g u"),
+            in_=w4s_raw[:].rearrange("p a (g u) -> p a g u", u=PACK),
+        )
+
+        kb_rows = keep.tile([P, J], F32, name="kb_rows")
+        for h in range(2):
+            spread = bank(h, "kb_bank%d" % h)
+            for e in range(PACK):
+                col = PACK * h + e
+                nc.tensor.transpose(spread[:, e * P : (e + 1) * P], kb_cols[:, col : col + 1].to_broadcast([P, P]), ident[:])
+            nc.scalar.copy(
+                out=kb_rows[:].rearrange("p (n e) -> p n e", e=J // P)[:, :, PACK * h : PACK * (h + 1)],
+                in_=spread[:].rearrange("p (e n) -> p n e", e=PACK),
+            )
+
+        c_mx = [[mx_tiles("c%d%d" % (a, h), HALF) for h in range(2)] for a in range(2)]
+        wk_mx = [mx_tiles("wk%d" % a, D) for a in range(2)]
+        x_mx = [[mx_tiles("x%d%d" % (a, h), HALF) for h in range(2)] for a in range(2)]
+        kc_codes, kc_scales = mx_tiles("kc", J)
+        kc_banks = {}
+
+        def half(h):
+            return slice(h * HALF, (h + 1) * HALF)
+
+        def kc_pass(a, h):
+            for u in range(PACK):
+                if a == 0:
+                    kc_banks[h, u] = bank(PACK * h + u, "kc_bank%d%d" % (h, u))
+                cols = slice(u * P, (u + 1) * P)
+                nc.tensor.matmul_mx(
+                    out=kc_banks[h, u][:],
+                    lhsT=wk_mx[a][0][:, cols].bitcast(FP8X4),
+                    lhsT_scale=wk_mx[a][1][:, cols],
+                    rhs=c_mx[a][h][0][:].bitcast(FP8X4),
+                    rhs_scale=c_mx[a][h][1][:],
+                    start=(a == 0),
+                    stop=(a == 1),
+                )
+
+        c00 = staged("c00")
+        c01 = staged("c01")
+        interleave("vector", c00, c_raw[0][:, :, half(0)], 0, GROUPS)
+        interleave("scalar", c01, c_raw[0][:, :, half(1)], 0, GROUPS)
+        quantize(c00[:], c_mx[0][0][0][:], c_mx[0][0][1][:])
+        kc_f32 = keep.tile([P, PACK, J], F32, name="kc_f32")
+
+        def kc_out(h):
+            for u in range(PACK):
+                nc.scalar.copy(out=kc_f32[:, u, half(h)], in_=kc_banks[h, u][:])
+
+        wk0 = staged("wk0")
+        interleave_dealt("vector", wk0, wk_raw[0][:], 0, GROUPS)
+        quantize(c01[:], c_mx[0][1][0][:], c_mx[0][1][1][:])
+        wk1 = staged("wk1")
+        interleave_dealt("vector", wk1, wk_raw[1][:], 0, GROUPS)
+        quantize(wk0[:], wk_mx[0][0][:], wk_mx[0][1][:])
+        kc_pass(0, 0)
+        quantize(wk1[:], wk_mx[1][0][:], wk_mx[1][1][:])
+        c10 = staged("c10")
+        interleave("vector", c10, c1_raw[0][:], 0, C_SPLIT)
+        interleave("scalar", c10, c1_raw[0][:], C_SPLIT, GROUPS)
+        quantize(c10[:], c_mx[1][0][0][:], c_mx[1][0][1][:])
+        kc_pass(1, 0)
+        kc_pass(0, 1)
+        kc_out(0)
+        c11 = staged("c11")
+        interleave("vector", c11, c1_raw[1][:], 0, GROUPS)
+        quantize(c11[:], c_mx[1][1][0][:], c_mx[1][1][1][:])
+        kc_pass(1, 1)
+        kc0 = staged("kc0")
+        interleave("vector", kc0, kc_f32[:, :, half(0)], 0, GROUPS)
+        kc_out(1)
+        nc.sync.dma_start(out=out_1.rearrange("(p t) j -> p t j", t=PACK), in_=kc_f32[:])
+
+        qr_banks = {}
+        qr_staged = {}
+        qr_mx = {}
+
+        def qr_pass(i, a):
+            h, cols = i // PACK, slice((i % PACK) * P, (i % PACK + 1) * P)
+            if a == 0:
+                qr_banks[i] = bank(i % PACK, "qr_bank%d" % i)
+            for u in range(PACK):
+                nc.tensor.matmul_mx(
+                    out=qr_banks[i][:, u * P : (u + 1) * P],
+                    lhsT=w4_codes[:, a, u, :].bitcast(FP4X4),
+                    lhsT_scale=w4_sc[:, a, u, :],
+                    rhs=x_mx[a][h][0][:, cols].bitcast(FP8X4),
+                    rhs_scale=x_mx[a][h][1][:, cols],
+                    start=(a == 0 and u == 0),
+                    stop=(a == 1 and u == PACK - 1),
+                )
+
+        def qr_out(i):
+            qr_staged[i] = small.tile([P, P * PACK], BF16, tag="qr_staged", name="qr_staged%d" % i, align_bytes=64)
+            nc.scalar.copy(
+                out=qr_staged[i][:].rearrange("p (m t) -> p m t", t=PACK),
+                in_=qr_banks[i][:].rearrange("p (t m) -> p m t", t=PACK),
+            )
+
+        def qr_quantize(i):
+            qr_mx[i] = mx_tiles("qr%d" % i, P)
+            quantize(qr_staged[i][:], qr_mx[i][0][:], qr_mx[i][1][:])
+
+        sc_banks = {}
+
+        def sc_matmul(i):
+            for h in range(2):
+                sc_banks[i, h] = bank(PACK + 2 * (i % 2) + h, "sc_bank%d%d" % (i, h))
+                nc.tensor.matmul_mx(
+                    out=sc_banks[i, h][:],
+                    lhsT=qr_mx[i][0][:].bitcast(FP8X4),
+                    lhsT_scale=qr_mx[i][1][:],
+                    rhs=kc_codes[:, half(h)].bitcast(FP8X4),
+                    rhs_scale=kc_scales[:, half(h)],
+                    start=True,
+                    stop=True,
+                )
+
+        def sc_out(i):
+            scores = keep.tile([P, J], F32, name="scores%d" % i)
+            for h in range(2):
+                nc.vector.scalar_tensor_tensor(
+                    out=scores[:, half(h)], in0=sc_banks[i, h][:], scalar=SCORE_SCALE, in1=kb_rows[:, half(h)], op0=ALU.mult, op1=ALU.add
+                )
+            nc.sync.dma_start(out=out_0[i * P : (i + 1) * P, :], in_=scores[:])
+
+        def xq(st, a, h, i0, i1):
+            quantize(st[:, i0 * HALF : i1 * HALF], x_mx[a][h][0][:, i0 * P : i1 * P], x_mx[a][h][1][:, i0 * P : i1 * P])
+
+        T = GROUPS // PACK
+        x00 = staged("x00")
+        x10 = staged("x10")
+        x01 = staged("x01")
+        x11 = staged("x11")
+        kc1 = staged("kc1")
+        interleave("vector", x00, x0_raw[:, :, half(0)], 0, 2 * T)
+        interleave("scalar", x00, x0_raw[:, :, half(0)], 2 * T, 4 * T)
+        quantize(kc0[:], kc_codes[:, half(0)], kc_scales[:, half(0)])
+        xq(x00, 0, 0, 0, 2)
+        qr_pass(0, 0)
+        qr_pass(1, 0)
+        interleave("vector", kc1, kc_f32[:, :, half(1)], 0, GROUPS)
+        interleave("vector", x10, x1_raw[0][:], 0, 2 * T)
+        interleave("scalar", x10, x1_raw[0][:], 2 * T, 4 * T)
+        xq(x00, 0, 0, 2, 4)
+        qr_pass(2, 0)
+        xq(x10, 1, 0, 0, 2)
+        qr_pass(0, 1)
+        qr_pass(1, 1)
+        qr_pass(3, 0)
+        interleave("scalar", x01, x0_raw[:, :, half(1)], 0, 2 * T)
+        quantize(kc1[:], kc_codes[:, half(1)], kc_scales[:, half(1)])
+        nc.sync.dma_start(out=out_2[0].rearrange("p j i -> p (j i)").bitcast(I32), in_=kc_codes[:].bitcast(I32))
+        for q in range(4):
+            nc.sync.dma_start(out=out_3[0, 4 * q : 4 * q + 4, :].bitcast(I32), in_=kc_scales[32 * q : 32 * q + 4, :].bitcast(I32))
+        xq(x10, 1, 0, 2, 4)
+        qr_pass(2, 1)
+        qr_pass(3, 1)
+        interleave("vector", x01, x0_raw[:, :, half(1)], 2 * T, 4 * T)
+        qr_out(0)
+        qr_out(1)
+        qr_quantize(0)
+        sc_matmul(0)
+        xq(x01, 0, 1, 0, 4)
+        qr_quantize(1)
+        sc_matmul(1)
+        interleave("scalar", x11, x1_raw[1][:], 0, 2 * T)
+        sc_out(0)
+        qr_out(2)
+        qr_out(3)
+        xq(x11, 1, 1, 0, 2)
+        qr_quantize(2)
+        sc_matmul(2)
+        for i in (4, 5):
+            qr_pass(i, 0)
+            qr_pass(i, 1)
+        interleave("scalar", x11, x1_raw[1][:], 2 * T, 4 * T)
+        sc_out(1)
+        qr_quantize(3)
+        sc_matmul(3)
+        qr_out(4)
+        qr_out(5)
+        xq(x11, 1, 1, 2, 4)
+        for i in (6, 7):
+            qr_pass(i, 0)
+            qr_pass(i, 1)
+        sc_out(2)
+        qr_quantize(4)
+        sc_matmul(4)
+        sc_out(3)
+        qr_quantize(5)
+        sc_matmul(5)
+        qr_out(6)
+        qr_out(7)
+        sc_out(4)
+        qr_quantize(6)
+        sc_matmul(6)
+        sc_out(5)
+        qr_quantize(7)
+        sc_matmul(7)
+        sc_out(6)
+        sc_out(7)

@@ -22,14 +22,16 @@ HALF = 512
 GROUPS = HALF // PACK
 SCORE_SCALE = 0.03125
 C_SPLIT = 84
-X_SPLIT = 64
+EARLY = 3
+V_TILES = 2
+FINE_FROM = 3
 
 
 def tile_mix_kvw_bias_kernel(tc, x, w4_words, w4_scales, c, wk, kb, out_0, out_1, out_2, out_3):
     nc = tc.nc
     with ExitStack() as ctx:
         keep = ctx.enter_context(tc.tile_pool(name="keep", bufs=1))
-        stage = ctx.enter_context(tc.tile_pool(name="stage", bufs=6))
+        stage = ctx.enter_context(tc.tile_pool(name="stage", bufs=4))
         small = ctx.enter_context(tc.tile_pool(name="small", bufs=4))
         psum = ctx.enter_context(tc.psum_pool(name="psum", bufs=1))
         ctx.enter_context(tc.manual_schedule())
@@ -74,10 +76,16 @@ def tile_mix_kvw_bias_kernel(tc, x, w4_words, w4_scales, c, wk, kb, out_0, out_1
         def quantize(src, codes, scales):
             nc.vector.quantize_mx(out=codes.bitcast(FP8X4), scales=scales, in_=src)
 
+        def quantize_halves(src, codes, scales):
+            for s in range(2):
+                cols = slice(s * HALF // 2, (s + 1) * HALF // 2)
+                quantize(src[:, s * 2 * HALF : (s + 1) * 2 * HALF], codes[:, cols], scales[:, cols])
+
         w4_raw = keep.tile([P, 2, 2 * D], U8, name="w4_raw")
         nc.sync.dma_start(out=w4_raw[:], in_=w4_words.rearrange("a p n -> p a n"))
         c_raw = [None, None]
         wk_raw = [None, None]
+        c_raw[0] = load_rows("c_raw0", c, 0, slice(0, J))
         w4s_raw = keep.tile([P, 2, D], U8, name="w4s_raw")
         nc.vector.memset(w4s_raw[:].bitcast(I32), 0)
         for q in range(4):
@@ -87,12 +95,11 @@ def tile_mix_kvw_bias_kernel(tc, x, w4_words, w4_scales, c, wk, kb, out_0, out_1
             )
         kb_cols = keep.tile([P, J // P], F32, name="kb_cols")
         nc.sync.dma_start(out=kb_cols[:], in_=kb.rearrange("(p e) -> p e", e=J // P))
-        c_raw[0] = load_rows("c_raw0", c, 0, slice(0, J))
         wk_raw[0] = load_rows("wk_raw0", wk, 0, slice(0, D))
         wk_raw[1] = load_rows("wk_raw1", wk, 1, slice(0, D))
         c1_raw = [load_rows("c_raw1_%d" % h, c, 1, slice(h * HALF, (h + 1) * HALF)) for h in range(2)]
         x0_raw = load_rows("x_raw0", x, 0, slice(0, M))
-        x1_raw = [load_rows("x_raw1_%d" % h, x, 1, slice(h * HALF, (h + 1) * HALF)) for h in range(2)]
+        x1_raw = [load_rows("x_raw1_0", x, 1, slice(0, EARLY * P)), load_rows("x_raw1_1", x, 1, slice(EARLY * P, M))]
 
         ident = keep.tile([P, P], F32, name="ident")
         make_identity(nc, ident[:])
@@ -105,25 +112,9 @@ def tile_mix_kvw_bias_kernel(tc, x, w4_words, w4_scales, c, wk, kb, out_0, out_1
                 in_=w4_raw[:, a].rearrange("p (g u b) -> p g u b", u=PACK, b=2),
             )
 
-        nc.vector.tensor_copy(
-            out=w4_sc[:].rearrange("p a u g -> p a g u"),
-            in_=w4s_raw[:].rearrange("p a (g u) -> p a g u", u=PACK),
-        )
-
-        kb_rows = keep.tile([P, J], F32, name="kb_rows")
-        for h in range(2):
-            spread = bank(h, "kb_bank%d" % h)
-            for e in range(PACK):
-                col = PACK * h + e
-                nc.tensor.transpose(spread[:, e * P : (e + 1) * P], kb_cols[:, col : col + 1].to_broadcast([P, P]), ident[:])
-            nc.scalar.copy(
-                out=kb_rows[:].rearrange("p (n e) -> p n e", e=J // P)[:, :, PACK * h : PACK * (h + 1)],
-                in_=spread[:].rearrange("p (e n) -> p n e", e=PACK),
-            )
 
         c_mx = [[mx_tiles("c%d%d" % (a, h), HALF) for h in range(2)] for a in range(2)]
         wk_mx = [mx_tiles("wk%d" % a, D) for a in range(2)]
-        x_mx = [[mx_tiles("x%d%d" % (a, h), HALF) for h in range(2)] for a in range(2)]
         kc_codes, kc_scales = mx_tiles("kc", J)
         kc_banks = {}
 
@@ -149,6 +140,10 @@ def tile_mix_kvw_bias_kernel(tc, x, w4_words, w4_scales, c, wk, kb, out_0, out_1
         c01 = staged("c01")
         interleave("vector", c00, c_raw[0][:, :, half(0)], 0, GROUPS)
         interleave("scalar", c01, c_raw[0][:, :, half(1)], 0, GROUPS)
+        nc.vector.tensor_copy(
+            out=w4_sc[:].rearrange("p a u g -> p a g u"),
+            in_=w4s_raw[:].rearrange("p a (g u) -> p a g u", u=PACK),
+        )
         quantize(c00[:], c_mx[0][0][0][:], c_mx[0][0][1][:])
         kc_f32 = keep.tile([P, PACK, J], F32, name="kc_f32")
 
@@ -157,7 +152,18 @@ def tile_mix_kvw_bias_kernel(tc, x, w4_words, w4_scales, c, wk, kb, out_0, out_1
                 nc.scalar.copy(out=kc_f32[:, u, half(h)], in_=kc_banks[h, u][:])
 
         wk0 = staged("wk0")
-        interleave_dealt("vector", wk0, wk_raw[0][:], 0, GROUPS)
+        interleave_dealt("scalar", wk0, wk_raw[0][:], 0, GROUPS)
+        kb_rows = keep.tile([P, J], F32, name="kb_rows")
+        for h in range(2):
+            spread = bank(6 + h, "kb_bank%d" % h)
+            for e in range(PACK):
+                col = PACK * h + e
+                nc.tensor.transpose(spread[:, e * P : (e + 1) * P], kb_cols[:, col : col + 1].to_broadcast([P, P]), ident[:])
+            nc.scalar.copy(
+                out=kb_rows[:].rearrange("p (n e) -> p n e", e=J // P)[:, :, PACK * h : PACK * (h + 1)],
+                in_=spread[:].rearrange("p (e n) -> p n e", e=PACK),
+            )
+
         quantize(c01[:], c_mx[0][1][0][:], c_mx[0][1][1][:])
         wk1 = staged("wk1")
         interleave_dealt("vector", wk1, wk_raw[1][:], 0, GROUPS)
@@ -165,27 +171,53 @@ def tile_mix_kvw_bias_kernel(tc, x, w4_words, w4_scales, c, wk, kb, out_0, out_1
         kc_pass(0, 0)
         quantize(wk1[:], wk_mx[1][0][:], wk_mx[1][1][:])
         c10 = staged("c10")
-        interleave("vector", c10, c1_raw[0][:], 0, C_SPLIT)
+        interleave("vector", c10, c1_raw[0][:], 0, GROUPS // 2)
+        interleave("vector", c10, c1_raw[0][:], GROUPS // 2, C_SPLIT)
         interleave("scalar", c10, c1_raw[0][:], C_SPLIT, GROUPS)
-        quantize(c10[:], c_mx[1][0][0][:], c_mx[1][0][1][:])
+        quantize_halves(c10, c_mx[1][0][0][:], c_mx[1][0][1][:])
         kc_pass(1, 0)
         kc_pass(0, 1)
         kc_out(0)
         c11 = staged("c11")
-        interleave("vector", c11, c1_raw[1][:], 0, GROUPS)
-        quantize(c11[:], c_mx[1][1][0][:], c_mx[1][1][1][:])
+        interleave("vector", c11, c1_raw[1][:], 0, GROUPS // 2)
+        interleave("vector", c11, c1_raw[1][:], GROUPS // 2, GROUPS)
+        quantize_halves(c11, c_mx[1][1][0][:], c_mx[1][1][1][:])
         kc_pass(1, 1)
         kc0 = staged("kc0")
-        interleave("vector", kc0, kc_f32[:, :, half(0)], 0, GROUPS)
+        interleave("vector", kc0, kc_f32[:, :, half(0)], 0, GROUPS // 2)
+        interleave("vector", kc0, kc_f32[:, :, half(0)], GROUPS // 2, GROUPS)
+        quantize_halves(kc0, kc_codes[:, half(0)], kc_scales[:, half(0)])
         kc_out(1)
         nc.sync.dma_start(out=out_1.rearrange("(p t) j -> p t j", t=PACK), in_=kc_f32[:])
+
+        x_staged = [keep.tile([P, 2 * HALF], BF16, name="x_staged%d" % i, align_bytes=64) for i in range(8)]
+        x_mx = [mx_tiles("x%d" % i, 2 * P) for i in range(8)]
+
+        def x_round(i, a):
+            if a == 0:
+                rows = x0_raw[:, :, i * P : (i + 1) * P]
+            elif i < EARLY:
+                rows = x1_raw[0][:, :, i * P : (i + 1) * P]
+            else:
+                rows = x1_raw[1][:, :, (i - EARLY) * P : (i - EARLY + 1) * P]
+            interleave("vector" if i < V_TILES else "scalar", x_staged[i][:, half(a)], rows, 0, P // PACK)
+
+        def qr_one(i, a):
+            cols = slice(a * P, (a + 1) * P)
+            quantize(x_staged[i][:, half(a)], x_mx[i][0][:, cols], x_mx[i][1][:, cols])
+            qr_pass(i, a)
+
+        def qr_both(i):
+            quantize(x_staged[i][:], x_mx[i][0][:], x_mx[i][1][:])
+            qr_pass(i, 0)
+            qr_pass(i, 1)
 
         qr_banks = {}
         qr_staged = {}
         qr_mx = {}
 
         def qr_pass(i, a):
-            h, cols = i // PACK, slice((i % PACK) * P, (i % PACK + 1) * P)
+            cols = slice(a * P, (a + 1) * P)
             if a == 0:
                 qr_banks[i] = bank(i % PACK, "qr_bank%d" % i)
             for u in range(PACK):
@@ -193,8 +225,8 @@ def tile_mix_kvw_bias_kernel(tc, x, w4_words, w4_scales, c, wk, kb, out_0, out_1
                     out=qr_banks[i][:, u * P : (u + 1) * P],
                     lhsT=w4_codes[:, a, u, :].bitcast(FP4X4),
                     lhsT_scale=w4_sc[:, a, u, :],
-                    rhs=x_mx[a][h][0][:, cols].bitcast(FP8X4),
-                    rhs_scale=x_mx[a][h][1][:, cols],
+                    rhs=x_mx[i][0][:, cols].bitcast(FP8X4),
+                    rhs_scale=x_mx[i][1][:, cols],
                     start=(a == 0 and u == 0),
                     stop=(a == 1 and u == PACK - 1),
                 )
@@ -225,87 +257,58 @@ def tile_mix_kvw_bias_kernel(tc, x, w4_words, w4_scales, c, wk, kb, out_0, out_1
                     stop=True,
                 )
 
-        def sc_out(i):
-            scores = keep.tile([P, J], F32, name="scores%d" % i)
-            for h in range(2):
+        scores_tiles = [keep.tile([P, J], F32, name="scores%d" % i) for i in range(8)]
+
+        def sc_half(i, h):
+            scores = scores_tiles[i]
+            if True:
                 nc.vector.scalar_tensor_tensor(
                     out=scores[:, half(h)], in0=sc_banks[i, h][:], scalar=SCORE_SCALE, in1=kb_rows[:, half(h)], op0=ALU.mult, op1=ALU.add
                 )
-            nc.sync.dma_start(out=out_0[i * P : (i + 1) * P, :], in_=scores[:])
+                if i >= FINE_FROM:
+                    nc.sync.dma_start(out=out_0[i * P : (i + 1) * P, half(h)], in_=scores[:, half(h)])
+            if i < FINE_FROM and h == 1:
+                nc.sync.dma_start(out=out_0[i * P : (i + 1) * P, :], in_=scores[:])
 
-        def xq(st, a, h, i0, i1):
-            quantize(st[:, i0 * HALF : i1 * HALF], x_mx[a][h][0][:, i0 * P : i1 * P], x_mx[a][h][1][:, i0 * P : i1 * P])
-
-        T = GROUPS // PACK
-        x00 = staged("x00")
-        x10 = staged("x10")
-        x01 = staged("x01")
-        x11 = staged("x11")
         kc1 = staged("kc1")
-        interleave("vector", x00, x0_raw[:, :, half(0)], 0, 2 * T)
-        interleave("scalar", x00, x0_raw[:, :, half(0)], 2 * T, 4 * T)
-        quantize(kc0[:], kc_codes[:, half(0)], kc_scales[:, half(0)])
-        xq(x00, 0, 0, 0, 2)
-        qr_pass(0, 0)
-        qr_pass(1, 0)
-        interleave("vector", kc1, kc_f32[:, :, half(1)], 0, GROUPS)
-        interleave("vector", x10, x1_raw[0][:], 0, 2 * T)
-        interleave("scalar", x10, x1_raw[0][:], 2 * T, 4 * T)
-        xq(x00, 0, 0, 2, 4)
-        qr_pass(2, 0)
-        xq(x10, 1, 0, 0, 2)
-        qr_pass(0, 1)
-        qr_pass(1, 1)
-        qr_pass(3, 0)
-        interleave("scalar", x01, x0_raw[:, :, half(1)], 0, 2 * T)
+        for i in range(4):
+            x_round(i, 0)
+        qr_one(0, 0)
+        qr_one(1, 0)
+        interleave("vector", kc1, kc_f32[:, :, half(1)], 0, 64)
+        x_round(0, 1)
+        x_round(1, 1)
+        x_round(2, 1)
+        qr_one(0, 1)
+        qr_one(2, 0)
+        qr_one(1, 1)
+        x_round(4, 0)
+        x_round(5, 0)
+        interleave("vector", kc1, kc_f32[:, :, half(1)], 64, GROUPS)
+        qr_out(0)
+        qr_one(2, 1)
+        qr_one(3, 0)
         quantize(kc1[:], kc_codes[:, half(1)], kc_scales[:, half(1)])
+        qr_quantize(0)
+        sc_matmul(0)
+        qr_out(1)
         nc.sync.dma_start(out=out_2[0].rearrange("p j i -> p (j i)").bitcast(I32), in_=kc_codes[:].bitcast(I32))
         for q in range(4):
             nc.sync.dma_start(out=out_3[0, 4 * q : 4 * q + 4, :].bitcast(I32), in_=kc_scales[32 * q : 32 * q + 4, :].bitcast(I32))
-        xq(x10, 1, 0, 2, 4)
-        qr_pass(2, 1)
-        qr_pass(3, 1)
-        interleave("vector", x01, x0_raw[:, :, half(1)], 2 * T, 4 * T)
-        qr_out(0)
-        qr_out(1)
-        qr_quantize(0)
-        sc_matmul(0)
-        xq(x01, 0, 1, 0, 4)
-        qr_quantize(1)
-        sc_matmul(1)
-        interleave("scalar", x11, x1_raw[1][:], 0, 2 * T)
-        sc_out(0)
-        qr_out(2)
-        qr_out(3)
-        xq(x11, 1, 1, 0, 2)
-        qr_quantize(2)
-        sc_matmul(2)
-        for i in (4, 5):
-            qr_pass(i, 0)
-            qr_pass(i, 1)
-        interleave("scalar", x11, x1_raw[1][:], 2 * T, 4 * T)
-        sc_out(1)
-        qr_quantize(3)
-        sc_matmul(3)
-        qr_out(4)
-        qr_out(5)
-        xq(x11, 1, 1, 2, 4)
-        for i in (6, 7):
-            qr_pass(i, 0)
-            qr_pass(i, 1)
-        sc_out(2)
-        qr_quantize(4)
-        sc_matmul(4)
-        sc_out(3)
-        qr_quantize(5)
-        sc_matmul(5)
-        qr_out(6)
-        qr_out(7)
-        sc_out(4)
-        qr_quantize(6)
-        sc_matmul(6)
-        sc_out(5)
-        qr_quantize(7)
-        sc_matmul(7)
-        sc_out(6)
-        sc_out(7)
+        x_round(3, 1)
+        for i in range(8):
+            if i + 1 < 8:
+                qr_quantize(i + 1)
+                sc_matmul(i + 1)
+            if i + 2 < 8:
+                qr_out(i + 2)
+            if i + 4 < 8:
+                x_round(i + 4, 1)
+            if i + 6 < 8:
+                x_round(i + 6, 0)
+            sc_half(i, 0)
+            if i == 0:
+                qr_one(3, 1)
+            elif i + 3 < 8:
+                qr_both(i + 3)
+            sc_half(i, 1)

@@ -18,32 +18,41 @@ ALU = mybir.AluOpType
 P = 128
 PACK = 4
 K_PASS = P * PACK
-HALF = 512
-GROUPS = HALF // PACK
+PASSES = K // K_PASS
+BANK = 512
+HALVES = J // BANK
+TILES = M // P
+QUADRANT = 32
 SCORE_SCALE = 0.03125
-C_SPLIT = 84
-EARLY = 3
-V_TILES = 2
-FINE_FROM = 3
+
+C_VECTOR = 336
+KC_FIRST = 128
+EARLY_TILES = 3
+VECTOR_TILES = 2
+HALF_STORES_FROM = 3
 
 
 def tile_mix_kvw_bias_kernel(tc, x, w4_words, w4_scales, c, wk, kb, out_0, out_1, out_2, out_3):
     nc = tc.nc
+    vector_copy = nc.vector.tensor_copy
+    scalar_copy = nc.scalar.copy
+
     with ExitStack() as ctx:
         keep = ctx.enter_context(tc.tile_pool(name="keep", bufs=1))
         stage = ctx.enter_context(tc.tile_pool(name="stage", bufs=4))
-        small = ctx.enter_context(tc.tile_pool(name="small", bufs=4))
         psum = ctx.enter_context(tc.psum_pool(name="psum", bufs=1))
         ctx.enter_context(tc.manual_schedule())
 
-        def bank(b, name):
-            return psum.tile([P, HALF], F32, tag="bank%d" % b, name=name)
+        def span(i, width):
+            return slice(i * width, (i + 1) * width)
 
-        def load_rows(name, src, a, cols):
-            width = cols.stop - cols.start
-            raw = keep.tile([P, PACK, width], F32, name=name)
-            nc.sync.dma_start(out=raw[:], in_=src[a * K_PASS : (a + 1) * K_PASS, cols].rearrange("(p t) w -> p t w", t=PACK))
-            return raw
+        def bank(b, name):
+            return psum.tile([P, BANK], F32, tag="bank%d" % b, name=name)
+
+        def load_pass(name, src, a, cols):
+            rows = keep.tile([P, PACK, cols.stop - cols.start], F32, name=name)
+            nc.sync.dma_start(out=rows[:], in_=src[span(a, K_PASS), cols].rearrange("(p t) w -> p t w", t=PACK))
+            return rows
 
         def mx_tiles(name, width):
             codes = keep.tile([P, width], U32, name=name + "_codes", align_bytes=64)
@@ -51,264 +60,220 @@ def tile_mix_kvw_bias_kernel(tc, x, w4_words, w4_scales, c, wk, kb, out_0, out_1
             return codes, scales
 
         def staged(name):
-            return stage.tile([P, HALF * PACK], BF16, tag="staged", name=name, align_bytes=64)
+            return stage.tile([P, BANK * PACK], BF16, tag="staged", name=name, align_bytes=64)
 
-        def copy_on(engine, dst, src):
-            if engine == "vector":
-                nc.vector.tensor_copy(out=dst, in_=src)
-            else:
-                nc.scalar.copy(out=dst, in_=src)
-
-        def interleave(engine, dst, rows, g0, g1):
-            copy_on(
-                engine,
-                dst[:].rearrange("p (g i t) -> p g t i", i=PACK, t=PACK)[:, g0:g1],
-                rows.rearrange("p t (g i) -> p g t i", i=PACK)[:, g0:g1],
+        def interleave(copy, dst, rows, w0, w1):
+            groups = slice(w0 // 4, w1 // 4)
+            copy(
+                out=dst.rearrange("p (g i t) -> p g t i", i=4, t=PACK)[:, groups],
+                in_=rows.rearrange("p t (g i) -> p g t i", i=4)[:, groups],
             )
 
-        def interleave_dealt(engine, dst, rows, g0, g1):
-            copy_on(
-                engine,
-                dst[:].rearrange("p (u g t) -> p g t u", u=PACK, t=PACK)[:, g0:g1],
-                rows.rearrange("p t (g u) -> p g t u", u=PACK)[:, g0:g1],
+        def interleave_dealt(copy, dst, rows):
+            for pair in range(PACK // 2):
+                copy(
+                    out=dst.rearrange("p (u g t) -> p g t u", u=PACK, t=PACK)[:, :, :, span(pair, 2)],
+                    in_=rows.rearrange("p t (g u) -> p g t u", u=PACK)[:, :, :, span(pair, 2)],
+                )
+
+        def quantize(src, mx, cols):
+            codes, scales = mx
+            nc.vector.quantize_mx(out=codes[:, cols].bitcast(FP8X4), scales=scales[:, cols], in_=src)
+
+        def matmul(out, lhsT, lhsT_scale, rhs_mx, rhs_cols, start, stop):
+            codes, scales = rhs_mx
+            nc.tensor.matmul_mx(
+                out=out, lhsT=lhsT, lhsT_scale=lhsT_scale, rhs=codes[:, rhs_cols].bitcast(FP8X4), rhs_scale=scales[:, rhs_cols],
+                start=start, stop=stop,
             )
 
-        def quantize(src, codes, scales):
-            nc.vector.quantize_mx(out=codes.bitcast(FP8X4), scales=scales, in_=src)
-
-        def quantize_halves(src, codes, scales):
-            for s in range(2):
-                cols = slice(s * HALF // 2, (s + 1) * HALF // 2)
-                quantize(src[:, s * 2 * HALF : (s + 1) * 2 * HALF], codes[:, cols], scales[:, cols])
-
-        w4_raw = keep.tile([P, 2, 2 * D], U8, name="w4_raw")
-        nc.sync.dma_start(out=w4_raw[:], in_=w4_words.rearrange("a p n -> p a n"))
-        c_raw = [None, None]
-        wk_raw = [None, None]
-        c_raw[0] = load_rows("c_raw0", c, 0, slice(0, J))
-        w4s_raw = keep.tile([P, 2, D], U8, name="w4s_raw")
-        nc.vector.memset(w4s_raw[:].bitcast(I32), 0)
-        for q in range(4):
+        w4_rows = keep.tile([P, PASSES, 2 * D], U8, name="w4_rows")
+        nc.sync.dma_start(out=w4_rows[:], in_=w4_words.rearrange("a p n -> p a n"))
+        c0_rows = load_pass("c0_rows", c, 0, slice(0, J))
+        w4_scale_rows = keep.tile([P, PASSES, D], U8, name="w4_scale_rows")
+        nc.vector.memset(w4_scale_rows[:].bitcast(I32), 0)
+        for q in range(P // QUADRANT):
             nc.sync.dma_start(
-                out=w4s_raw[32 * q : 32 * q + 4].bitcast(I32),
-                in_=w4_scales[:, 4 * q : 4 * q + 4, :].rearrange("a r n -> r a n").bitcast(I32),
+                out=w4_scale_rows[QUADRANT * q : QUADRANT * q + 4].bitcast(I32),
+                in_=w4_scales[:, span(q, 4), :].rearrange("a r n -> r a n").bitcast(I32),
             )
         kb_cols = keep.tile([P, J // P], F32, name="kb_cols")
         nc.sync.dma_start(out=kb_cols[:], in_=kb.rearrange("(p e) -> p e", e=J // P))
-        wk_raw[0] = load_rows("wk_raw0", wk, 0, slice(0, D))
-        wk_raw[1] = load_rows("wk_raw1", wk, 1, slice(0, D))
-        c1_raw = [load_rows("c_raw1_%d" % h, c, 1, slice(h * HALF, (h + 1) * HALF)) for h in range(2)]
-        x0_raw = load_rows("x_raw0", x, 0, slice(0, M))
-        x1_raw = [load_rows("x_raw1_0", x, 1, slice(0, EARLY * P)), load_rows("x_raw1_1", x, 1, slice(EARLY * P, M))]
+        wk_rows = [load_pass("wk%d_rows" % a, wk, a, slice(0, D)) for a in range(PASSES)]
+        c1_rows = [load_pass("c1%d_rows" % h, c, 1, span(h, BANK)) for h in range(HALVES)]
+        x0_rows = load_pass("x0_rows", x, 0, slice(0, M))
+        x1_early = load_pass("x1_early", x, 1, slice(0, EARLY_TILES * P))
+        x1_late = load_pass("x1_late", x, 1, slice(EARLY_TILES * P, M))
 
         ident = keep.tile([P, P], F32, name="ident")
         make_identity(nc, ident[:])
 
-        w4_codes = keep.tile([P, 2, PACK, 2 * P], U8, name="w4_codes", align_bytes=64)
-        w4_sc = keep.tile([P, 2, PACK, P], U8, name="w4_sc", align_bytes=64)
-        for a in range(2):
-            nc.vector.tensor_copy(
-                out=w4_codes[:, a].rearrange("p u (g b) -> p g u b", b=2),
-                in_=w4_raw[:, a].rearrange("p (g u b) -> p g u b", u=PACK, b=2),
+        w4_codes = keep.tile([P, PASSES, PACK, 2 * P], U8, name="w4_codes", align_bytes=64)
+        w4_planes = keep.tile([P, PASSES, PACK, P], U8, name="w4_planes", align_bytes=64)
+        for a in range(PASSES):
+            vector_copy(
+                out=w4_codes[:, a].rearrange("p u (g b) -> p u g b", b=2),
+                in_=w4_rows[:, a].rearrange("p (g u b) -> p u g b", u=PACK, b=2),
             )
 
-
-        c_mx = [[mx_tiles("c%d%d" % (a, h), HALF) for h in range(2)] for a in range(2)]
-        wk_mx = [mx_tiles("wk%d" % a, D) for a in range(2)]
-        kc_codes, kc_scales = mx_tiles("kc", J)
+        c_mx = [[mx_tiles("c%d%d" % (a, h), BANK) for h in range(HALVES)] for a in range(PASSES)]
+        wk_mx = [mx_tiles("wk%d" % a, D) for a in range(PASSES)]
+        kc_mx = mx_tiles("kc", J)
+        kc_f32 = keep.tile([P, PACK, J], F32, name="kc_f32")
         kc_banks = {}
-
-        def half(h):
-            return slice(h * HALF, (h + 1) * HALF)
+        whole = slice(0, BANK)
 
         def kc_pass(a, h):
+            codes, scales = wk_mx[a]
             for u in range(PACK):
                 if a == 0:
                     kc_banks[h, u] = bank(PACK * h + u, "kc_bank%d%d" % (h, u))
-                cols = slice(u * P, (u + 1) * P)
-                nc.tensor.matmul_mx(
-                    out=kc_banks[h, u][:],
-                    lhsT=wk_mx[a][0][:, cols].bitcast(FP8X4),
-                    lhsT_scale=wk_mx[a][1][:, cols],
-                    rhs=c_mx[a][h][0][:].bitcast(FP8X4),
-                    rhs_scale=c_mx[a][h][1][:],
-                    start=(a == 0),
-                    stop=(a == 1),
-                )
-
-        c00 = staged("c00")
-        c01 = staged("c01")
-        interleave("vector", c00, c_raw[0][:, :, half(0)], 0, GROUPS)
-        interleave("scalar", c01, c_raw[0][:, :, half(1)], 0, GROUPS)
-        nc.vector.tensor_copy(
-            out=w4_sc[:].rearrange("p a u g -> p a g u"),
-            in_=w4s_raw[:].rearrange("p a (g u) -> p a g u", u=PACK),
-        )
-        quantize(c00[:], c_mx[0][0][0][:], c_mx[0][0][1][:])
-        kc_f32 = keep.tile([P, PACK, J], F32, name="kc_f32")
+                matmul(kc_banks[h, u][:], codes[:, span(u, P)].bitcast(FP8X4), scales[:, span(u, P)], c_mx[a][h], whole, a == 0, a == PASSES - 1)
 
         def kc_out(h):
             for u in range(PACK):
-                nc.scalar.copy(out=kc_f32[:, u, half(h)], in_=kc_banks[h, u][:])
+                scalar_copy(out=kc_f32[:, u, span(h, BANK)], in_=kc_banks[h, u][:])
 
+        c00, c01 = staged("c00"), staged("c01")
+        interleave(vector_copy, c00[:], c0_rows[:, :, span(0, BANK)], 0, BANK)
+        interleave(scalar_copy, c01[:], c0_rows[:, :, span(1, BANK)], 0, BANK)
+        vector_copy(out=w4_planes[:], in_=w4_scale_rows[:].rearrange("p a (g u) -> p a u g", u=PACK))
+        quantize(c00[:], c_mx[0][0], whole)
         wk0 = staged("wk0")
-        interleave_dealt("scalar", wk0, wk_raw[0][:], 0, GROUPS)
+        interleave_dealt(scalar_copy, wk0[:], wk_rows[0][:])
+
         kb_rows = keep.tile([P, J], F32, name="kb_rows")
-        for h in range(2):
-            spread = bank(6 + h, "kb_bank%d" % h)
-            for e in range(PACK):
-                col = PACK * h + e
-                nc.tensor.transpose(spread[:, e * P : (e + 1) * P], kb_cols[:, col : col + 1].to_broadcast([P, P]), ident[:])
-            nc.scalar.copy(
-                out=kb_rows[:].rearrange("p (n e) -> p n e", e=J // P)[:, :, PACK * h : PACK * (h + 1)],
-                in_=spread[:].rearrange("p (e n) -> p n e", e=PACK),
+        for s in range(2):
+            spread = bank(6 + s, "kb_bank%d" % s)
+            for e in range(4):
+                nc.tensor.transpose(spread[:, span(e, P)], kb_cols[:, span(4 * s + e, 1)].to_broadcast([P, P]), ident[:])
+            scalar_copy(
+                out=kb_rows[:].rearrange("p (n e) -> p n e", e=J // P)[:, :, span(s, 4)],
+                in_=spread[:].rearrange("p (e n) -> p n e", e=4),
             )
 
-        quantize(c01[:], c_mx[0][1][0][:], c_mx[0][1][1][:])
+        quantize(c01[:], c_mx[0][1], whole)
         wk1 = staged("wk1")
-        interleave_dealt("vector", wk1, wk_raw[1][:], 0, GROUPS)
-        quantize(wk0[:], wk_mx[0][0][:], wk_mx[0][1][:])
+        interleave_dealt(vector_copy, wk1[:], wk_rows[1][:])
+        quantize(wk0[:], wk_mx[0], whole)
         kc_pass(0, 0)
-        quantize(wk1[:], wk_mx[1][0][:], wk_mx[1][1][:])
+        quantize(wk1[:], wk_mx[1], whole)
         c10 = staged("c10")
-        interleave("vector", c10, c1_raw[0][:], 0, GROUPS // 2)
-        interleave("vector", c10, c1_raw[0][:], GROUPS // 2, C_SPLIT)
-        interleave("scalar", c10, c1_raw[0][:], C_SPLIT, GROUPS)
-        quantize_halves(c10, c_mx[1][0][0][:], c_mx[1][0][1][:])
+        interleave(vector_copy, c10[:], c1_rows[0][:], 0, C_VECTOR)
+        interleave(scalar_copy, c10[:], c1_rows[0][:], C_VECTOR, BANK)
+        quantize(c10[:], c_mx[1][0], whole)
         kc_pass(1, 0)
         kc_pass(0, 1)
         kc_out(0)
         c11 = staged("c11")
-        interleave("vector", c11, c1_raw[1][:], 0, GROUPS // 2)
-        interleave("vector", c11, c1_raw[1][:], GROUPS // 2, GROUPS)
-        quantize_halves(c11, c_mx[1][1][0][:], c_mx[1][1][1][:])
+        interleave(vector_copy, c11[:], c1_rows[1][:], 0, BANK)
+        quantize(c11[:], c_mx[1][1], whole)
         kc_pass(1, 1)
         kc0 = staged("kc0")
-        interleave("vector", kc0, kc_f32[:, :, half(0)], 0, GROUPS // 2)
-        interleave("vector", kc0, kc_f32[:, :, half(0)], GROUPS // 2, GROUPS)
-        quantize_halves(kc0, kc_codes[:, half(0)], kc_scales[:, half(0)])
+        interleave(vector_copy, kc0[:], kc_f32[:, :, span(0, BANK)], 0, BANK)
         kc_out(1)
         nc.sync.dma_start(out=out_1.rearrange("(p t) j -> p t j", t=PACK), in_=kc_f32[:])
 
-        x_staged = [keep.tile([P, 2 * HALF], BF16, name="x_staged%d" % i, align_bytes=64) for i in range(8)]
-        x_mx = [mx_tiles("x%d" % i, 2 * P) for i in range(8)]
+        x_staged = [keep.tile([P, PASSES * K_PASS], BF16, name="x_staged%d" % i, align_bytes=64) for i in range(TILES)]
+        x_mx = [mx_tiles("x%d" % i, PASSES * P) for i in range(TILES)]
+        qr_staged = [keep.tile([P, K_PASS], BF16, name="qr_staged%d" % i, align_bytes=64) for i in range(TILES)]
+        qr_mx = [mx_tiles("qr%d" % i, P) for i in range(TILES)]
+        scores = [keep.tile([P, J], F32, name="scores%d" % i) for i in range(TILES)]
+        qr_banks = {}
+        sc_banks = {}
 
         def x_round(i, a):
             if a == 0:
-                rows = x0_raw[:, :, i * P : (i + 1) * P]
-            elif i < EARLY:
-                rows = x1_raw[0][:, :, i * P : (i + 1) * P]
+                rows = x0_rows[:, :, span(i, P)]
+            elif i < EARLY_TILES:
+                rows = x1_early[:, :, span(i, P)]
             else:
-                rows = x1_raw[1][:, :, (i - EARLY) * P : (i - EARLY + 1) * P]
-            interleave("vector" if i < V_TILES else "scalar", x_staged[i][:, half(a)], rows, 0, P // PACK)
-
-        def qr_one(i, a):
-            cols = slice(a * P, (a + 1) * P)
-            quantize(x_staged[i][:, half(a)], x_mx[i][0][:, cols], x_mx[i][1][:, cols])
-            qr_pass(i, a)
-
-        def qr_both(i):
-            quantize(x_staged[i][:], x_mx[i][0][:], x_mx[i][1][:])
-            qr_pass(i, 0)
-            qr_pass(i, 1)
-
-        qr_banks = {}
-        qr_staged = {}
-        qr_mx = {}
+                rows = x1_late[:, :, span(i - EARLY_TILES, P)]
+            interleave(vector_copy if i < VECTOR_TILES else scalar_copy, x_staged[i][:, span(a, K_PASS)], rows, 0, P)
 
         def qr_pass(i, a):
-            cols = slice(a * P, (a + 1) * P)
             if a == 0:
-                qr_banks[i] = bank(i % PACK, "qr_bank%d" % i)
+                qr_banks[i] = bank(i % 4, "qr_bank%d" % i)
             for u in range(PACK):
-                nc.tensor.matmul_mx(
-                    out=qr_banks[i][:, u * P : (u + 1) * P],
-                    lhsT=w4_codes[:, a, u, :].bitcast(FP4X4),
-                    lhsT_scale=w4_sc[:, a, u, :],
-                    rhs=x_mx[i][0][:, cols].bitcast(FP8X4),
-                    rhs_scale=x_mx[i][1][:, cols],
-                    start=(a == 0 and u == 0),
-                    stop=(a == 1 and u == PACK - 1),
+                matmul(
+                    qr_banks[i][:, span(u, P)], w4_codes[:, a, u, :].bitcast(FP4X4), w4_planes[:, a, u, :], x_mx[i], span(a, P),
+                    a == 0 and u == 0, a == PASSES - 1 and u == PACK - 1,
                 )
 
+        def qr_one_pass(i, a):
+            quantize(x_staged[i][:, span(a, K_PASS)], x_mx[i], span(a, P))
+            qr_pass(i, a)
+
+        def qr_both_passes(i):
+            quantize(x_staged[i][:], x_mx[i], slice(0, PASSES * P))
+            for a in range(PASSES):
+                qr_pass(i, a)
+
         def qr_out(i):
-            qr_staged[i] = small.tile([P, P * PACK], BF16, tag="qr_staged", name="qr_staged%d" % i, align_bytes=64)
-            nc.scalar.copy(
+            scalar_copy(
                 out=qr_staged[i][:].rearrange("p (m t) -> p m t", t=PACK),
                 in_=qr_banks[i][:].rearrange("p (t m) -> p m t", t=PACK),
             )
 
         def qr_quantize(i):
-            qr_mx[i] = mx_tiles("qr%d" % i, P)
-            quantize(qr_staged[i][:], qr_mx[i][0][:], qr_mx[i][1][:])
-
-        sc_banks = {}
+            quantize(qr_staged[i][:], qr_mx[i], slice(0, P))
 
         def sc_matmul(i):
-            for h in range(2):
-                sc_banks[i, h] = bank(PACK + 2 * (i % 2) + h, "sc_bank%d%d" % (i, h))
-                nc.tensor.matmul_mx(
-                    out=sc_banks[i, h][:],
-                    lhsT=qr_mx[i][0][:].bitcast(FP8X4),
-                    lhsT_scale=qr_mx[i][1][:],
-                    rhs=kc_codes[:, half(h)].bitcast(FP8X4),
-                    rhs_scale=kc_scales[:, half(h)],
-                    start=True,
-                    stop=True,
-                )
+            codes, scales = qr_mx[i]
+            for h in range(HALVES):
+                sc_banks[i, h] = bank(4 + 2 * (i % 2) + h, "sc_bank%d%d" % (i, h))
+                matmul(sc_banks[i, h][:], codes[:].bitcast(FP8X4), scales[:], kc_mx, span(h, BANK), True, True)
 
-        scores_tiles = [keep.tile([P, J], F32, name="scores%d" % i) for i in range(8)]
-
-        def sc_half(i, h):
-            scores = scores_tiles[i]
-            if True:
-                nc.vector.scalar_tensor_tensor(
-                    out=scores[:, half(h)], in0=sc_banks[i, h][:], scalar=SCORE_SCALE, in1=kb_rows[:, half(h)], op0=ALU.mult, op1=ALU.add
-                )
-                if i >= FINE_FROM:
-                    nc.sync.dma_start(out=out_0[i * P : (i + 1) * P, half(h)], in_=scores[:, half(h)])
-            if i < FINE_FROM and h == 1:
-                nc.sync.dma_start(out=out_0[i * P : (i + 1) * P, :], in_=scores[:])
+        def sc_out(i, h):
+            cols = span(h, BANK)
+            nc.vector.scalar_tensor_tensor(
+                out=scores[i][:, cols], in0=sc_banks[i, h][:], scalar=SCORE_SCALE, in1=kb_rows[:, cols], op0=ALU.mult, op1=ALU.add
+            )
+            if i >= HALF_STORES_FROM:
+                nc.sync.dma_start(out=out_0[span(i, P), cols], in_=scores[i][:, cols])
+            elif h == HALVES - 1:
+                nc.sync.dma_start(out=out_0[span(i, P), :], in_=scores[i][:])
 
         kc1 = staged("kc1")
+        kc1_rows = kc_f32[:, :, span(1, BANK)]
         for i in range(4):
             x_round(i, 0)
-        qr_one(0, 0)
-        qr_one(1, 0)
-        interleave("vector", kc1, kc_f32[:, :, half(1)], 0, 64)
-        x_round(0, 1)
-        x_round(1, 1)
-        x_round(2, 1)
-        qr_one(0, 1)
-        qr_one(2, 0)
-        qr_one(1, 1)
+        quantize(kc0[:], kc_mx, span(0, BANK))
+        qr_one_pass(0, 0)
+        qr_one_pass(1, 0)
+        interleave(vector_copy, kc1[:], kc1_rows, 0, KC_FIRST)
+        for i in range(EARLY_TILES):
+            x_round(i, 1)
+        qr_one_pass(0, 1)
+        qr_one_pass(2, 0)
+        qr_one_pass(1, 1)
         x_round(4, 0)
-        x_round(5, 0)
-        interleave("vector", kc1, kc_f32[:, :, half(1)], 64, GROUPS)
+        interleave(vector_copy, kc1[:], kc1_rows, KC_FIRST, BANK)
         qr_out(0)
-        qr_one(2, 1)
-        qr_one(3, 0)
-        quantize(kc1[:], kc_codes[:, half(1)], kc_scales[:, half(1)])
+        qr_one_pass(2, 1)
+        qr_one_pass(3, 0)
         qr_quantize(0)
+        quantize(kc1[:], kc_mx, span(1, BANK))
         sc_matmul(0)
         qr_out(1)
-        nc.sync.dma_start(out=out_2[0].rearrange("p j i -> p (j i)").bitcast(I32), in_=kc_codes[:].bitcast(I32))
-        for q in range(4):
-            nc.sync.dma_start(out=out_3[0, 4 * q : 4 * q + 4, :].bitcast(I32), in_=kc_scales[32 * q : 32 * q + 4, :].bitcast(I32))
+        nc.sync.dma_start(out=out_2[0].rearrange("p j i -> p (j i)").bitcast(I32), in_=kc_mx[0][:].bitcast(I32))
+        for q in range(P // QUADRANT):
+            nc.sync.dma_start(out=out_3[0, span(q, 4), :].bitcast(I32), in_=kc_mx[1][QUADRANT * q : QUADRANT * q + 4, :].bitcast(I32))
         x_round(3, 1)
-        for i in range(8):
-            if i + 1 < 8:
+
+        for i in range(TILES):
+            if i + 1 < TILES:
                 qr_quantize(i + 1)
                 sc_matmul(i + 1)
-            if i + 2 < 8:
+            if i + 2 < TILES:
                 qr_out(i + 2)
-            if i + 4 < 8:
+            if i + 4 < TILES:
                 x_round(i + 4, 1)
-            if i + 6 < 8:
-                x_round(i + 6, 0)
-            sc_half(i, 0)
+            if i + 5 < TILES:
+                x_round(i + 5, 0)
+            sc_out(i, 0)
             if i == 0:
-                qr_one(3, 1)
-            elif i + 3 < 8:
-                qr_both(i + 3)
-            sc_half(i, 1)
+                qr_one_pass(3, 1)
+            elif i + 3 < TILES:
+                qr_both_passes(i + 3)
+            sc_out(i, 1)

@@ -26,10 +26,10 @@ QUADRANT = 32
 SCORE_SCALE = 0.03125
 
 C_VECTOR = 336
-KC_FIRST = 128
-EARLY_TILES = 3
+EARLY_TILES = 4
+BY_PASS_TILES = 3
 VECTOR_TILES = 2
-HALF_STORES_FROM = 3
+HALF_STORES_FROM = 5
 
 
 def tile_mix_kvw_bias_kernel(tc, x, w4_words, w4_scales, c, wk, kb, out_0, out_1, out_2, out_3):
@@ -101,9 +101,8 @@ def tile_mix_kvw_bias_kernel(tc, x, w4_words, w4_scales, c, wk, kb, out_0, out_1
         nc.sync.dma_start(out=kb_cols[:], in_=kb.rearrange("(p e) -> p e", e=J // P))
         wk_rows = [load_pass("wk%d_rows" % a, wk, a, slice(0, D)) for a in range(PASSES)]
         c1_rows = [load_pass("c1%d_rows" % h, c, 1, span(h, BANK)) for h in range(HALVES)]
-        x0_rows = load_pass("x0_rows", x, 0, slice(0, M))
-        x1_early = load_pass("x1_early", x, 1, slice(0, EARLY_TILES * P))
-        x1_late = load_pass("x1_late", x, 1, slice(EARLY_TILES * P, M))
+        x_early = [load_pass("x%d_early" % a, x, a, slice(0, EARLY_TILES * P)) for a in range(PASSES)]
+        x_late = [load_pass("x%d_late" % a, x, a, slice(EARLY_TILES * P, M)) for a in range(PASSES)]
 
         ident = keep.tile([P, P], F32, name="ident")
         make_identity(nc, ident[:])
@@ -169,10 +168,6 @@ def tile_mix_kvw_bias_kernel(tc, x, w4_words, w4_scales, c, wk, kb, out_0, out_1
         interleave(vector_copy, c11[:], c1_rows[1][:], 0, BANK)
         quantize(c11[:], c_mx[1][1], whole)
         kc_pass(1, 1)
-        kc0 = staged("kc0")
-        interleave(vector_copy, kc0[:], kc_f32[:, :, span(0, BANK)], 0, BANK)
-        kc_out(1)
-        nc.sync.dma_start(out=out_1.rearrange("(p t) j -> p t j", t=PACK), in_=kc_f32[:])
 
         x_staged = [keep.tile([P, PASSES * K_PASS], BF16, name="x_staged%d" % i, align_bytes=64) for i in range(TILES)]
         x_mx = [mx_tiles("x%d" % i, PASSES * P) for i in range(TILES)]
@@ -183,12 +178,10 @@ def tile_mix_kvw_bias_kernel(tc, x, w4_words, w4_scales, c, wk, kb, out_0, out_1
         sc_banks = {}
 
         def x_round(i, a):
-            if a == 0:
-                rows = x0_rows[:, :, span(i, P)]
-            elif i < EARLY_TILES:
-                rows = x1_early[:, :, span(i, P)]
+            if i < EARLY_TILES:
+                rows = x_early[a][:, :, span(i, P)]
             else:
-                rows = x1_late[:, :, span(i - EARLY_TILES, P)]
+                rows = x_late[a][:, :, span(i - EARLY_TILES, P)]
             interleave(vector_copy if i < VECTOR_TILES else scalar_copy, x_staged[i][:, span(a, K_PASS)], rows, 0, P)
 
         def qr_pass(i, a):
@@ -234,24 +227,25 @@ def tile_mix_kvw_bias_kernel(tc, x, w4_words, w4_scales, c, wk, kb, out_0, out_1
             elif h == HALVES - 1:
                 nc.sync.dma_start(out=out_0[span(i, P), :], in_=scores[i][:])
 
-        kc1 = staged("kc1")
-        kc1_rows = kc_f32[:, :, span(1, BANK)]
-        for i in range(4):
+        kc0, kc1 = staged("kc0"), staged("kc1")
+        for i in range(BY_PASS_TILES):
             x_round(i, 0)
-        quantize(kc0[:], kc_mx, span(0, BANK))
+        interleave(vector_copy, kc0[:], kc_f32[:, :, span(0, BANK)], 0, BANK)
+        kc_out(1)
+        nc.sync.dma_start(out=out_1.rearrange("(p t) j -> p t j", t=PACK), in_=kc_f32[:])
         qr_one_pass(0, 0)
         qr_one_pass(1, 0)
-        interleave(vector_copy, kc1[:], kc1_rows, 0, KC_FIRST)
-        for i in range(EARLY_TILES):
+        quantize(kc0[:], kc_mx, span(0, BANK))
+        for i in range(BY_PASS_TILES):
             x_round(i, 1)
-        qr_one_pass(0, 1)
+        for a in range(PASSES):
+            x_round(BY_PASS_TILES, a)
         qr_one_pass(2, 0)
+        qr_one_pass(0, 1)
         qr_one_pass(1, 1)
-        x_round(4, 0)
-        interleave(vector_copy, kc1[:], kc1_rows, KC_FIRST, BANK)
+        interleave(vector_copy, kc1[:], kc_f32[:, :, span(1, BANK)], 0, BANK)
         qr_out(0)
         qr_one_pass(2, 1)
-        qr_one_pass(3, 0)
         qr_quantize(0)
         quantize(kc1[:], kc_mx, span(1, BANK))
         sc_matmul(0)
@@ -259,8 +253,7 @@ def tile_mix_kvw_bias_kernel(tc, x, w4_words, w4_scales, c, wk, kb, out_0, out_1
         nc.sync.dma_start(out=out_2[0].rearrange("p j i -> p (j i)").bitcast(I32), in_=kc_mx[0][:].bitcast(I32))
         for q in range(P // QUADRANT):
             nc.sync.dma_start(out=out_3[0, span(q, 4), :].bitcast(I32), in_=kc_mx[1][QUADRANT * q : QUADRANT * q + 4, :].bitcast(I32))
-        x_round(3, 1)
-
+        x_round(4, 0)
         for i in range(TILES):
             if i + 1 < TILES:
                 qr_quantize(i + 1)
@@ -272,8 +265,6 @@ def tile_mix_kvw_bias_kernel(tc, x, w4_words, w4_scales, c, wk, kb, out_0, out_1
             if i + 5 < TILES:
                 x_round(i + 5, 0)
             sc_out(i, 0)
-            if i == 0:
-                qr_one_pass(3, 1)
-            elif i + 3 < TILES:
+            if i + 3 < TILES:
                 qr_both_passes(i + 3)
             sc_out(i, 1)

from contextlib import ExitStack

import concourse.mybir as mybir
from concourse.masks import make_identity

K, D, M, J = 1024, 512, 1024, 1024
FLOPS = 2 * K * D * M + 2 * K * D * J + 2 * D * M * J

F32 = mybir.dt.float32
BF16 = mybir.dt.bfloat16
I32 = mybir.dt.int32
U32 = mybir.dt.uint32
U8 = mybir.dt.uint8
FP8X4 = mybir.dt.float8_e4m3fn_x4
FP4X4 = mybir.dt.float4_e2m1fn_x4
ALU = mybir.AluOpType

P = 128
PACK = 4
K_PASS = P * PACK
PASSES = K // K_PASS
BANK = 512
HALVES = J // BANK
TILES = M // P
QUADRANT = 32
SCORE_SCALE = 0.03125

C_VECTOR = 336
EARLY_TILES = 4
BY_PASS_TILES = 3
VECTOR_TILES = 2
HALF_STORES_FROM = 5


def tile_mix_kvw_bias_kernel(tc, x, w4_words, w4_scales, c, wk, kb, out_0, out_1, out_2, out_3):
    nc = tc.nc
    vector_copy = nc.vector.tensor_copy
    scalar_copy = nc.scalar.copy

    with ExitStack() as ctx:
        keep = ctx.enter_context(tc.tile_pool(name="keep", bufs=1))
        stage = ctx.enter_context(tc.tile_pool(name="stage", bufs=4))
        psum = ctx.enter_context(tc.psum_pool(name="psum", bufs=1))
        ctx.enter_context(tc.manual_schedule())

        def span(i, width):
            return slice(i * width, (i + 1) * width)

        def bank(b, name):
            return psum.tile([P, BANK], F32, tag="bank%d" % b, name=name)

        def load_pass(name, src, a, cols):
            rows = keep.tile([P, PACK, cols.stop - cols.start], F32, name=name)
            nc.sync.dma_start(out=rows[:], in_=src[span(a, K_PASS), cols].rearrange("(p t) w -> p t w", t=PACK))
            return rows

        def mx_tiles(name, width):
            codes = keep.tile([P, width], U32, name=name + "_codes", align_bytes=64)
            scales = keep.tile([P, width], U8, name=name + "_scales", align_bytes=64)
            return codes, scales

        def staged(name):
            return stage.tile([P, BANK * PACK], BF16, tag="staged", name=name, align_bytes=64)

        def interleave(copy, dst, rows, w0, w1):
            groups = slice(w0 // 4, w1 // 4)
            copy(
                out=dst.rearrange("p (g i t) -> p g t i", i=4, t=PACK)[:, groups],
                in_=rows.rearrange("p t (g i) -> p g t i", i=4)[:, groups],
            )

        def interleave_dealt(copy, dst, rows):
            for pair in range(PACK // 2):
                copy(
                    out=dst.rearrange("p (u g t) -> p g t u", u=PACK, t=PACK)[:, :, :, span(pair, 2)],
                    in_=rows.rearrange("p t (g u) -> p g t u", u=PACK)[:, :, :, span(pair, 2)],
                )

        def quantize(src, mx, cols):
            codes, scales = mx
            nc.vector.quantize_mx(out=codes[:, cols].bitcast(FP8X4), scales=scales[:, cols], in_=src)

        def matmul(out, lhsT, lhsT_scale, rhs_mx, rhs_cols, start, stop):
            codes, scales = rhs_mx
            nc.tensor.matmul_mx(
                out=out, lhsT=lhsT, lhsT_scale=lhsT_scale, rhs=codes[:, rhs_cols].bitcast(FP8X4), rhs_scale=scales[:, rhs_cols],
                start=start, stop=stop,
            )

        w4_rows = keep.tile([P, PASSES, 2 * D], U8, name="w4_rows")
        nc.sync.dma_start(out=w4_rows[:], in_=w4_words.rearrange("a p n -> p a n"))
        c0_rows = load_pass("c0_rows", c, 0, slice(0, J))
        w4_scale_rows = keep.tile([P, PASSES, D], U8, name="w4_scale_rows")
        nc.vector.memset(w4_scale_rows[:].bitcast(I32), 0)
        for q in range(P // QUADRANT):
            nc.sync.dma_start(
                out=w4_scale_rows[QUADRANT * q : QUADRANT * q + 4].bitcast(I32),
                in_=w4_scales[:, span(q, 4), :].rearrange("a r n -> r a n").bitcast(I32),
            )
        kb_cols = keep.tile([P, J // P], F32, name="kb_cols")
        nc.sync.dma_start(out=kb_cols[:], in_=kb.rearrange("(p e) -> p e", e=J // P))
        wk_rows = [load_pass("wk%d_rows" % a, wk, a, slice(0, D)) for a in range(PASSES)]
        c1_rows = [load_pass("c1%d_rows" % h, c, 1, span(h, BANK)) for h in range(HALVES)]
        x_early = [load_pass("x%d_early" % a, x, a, slice(0, EARLY_TILES * P)) for a in range(PASSES)]
        x_late = [load_pass("x%d_late" % a, x, a, slice(EARLY_TILES * P, M)) for a in range(PASSES)]

        ident = keep.tile([P, P], F32, name="ident")
        make_identity(nc, ident[:])

        w4_codes = keep.tile([P, PASSES, PACK, 2 * P], U8, name="w4_codes", align_bytes=64)
        w4_planes = keep.tile([P, PASSES, PACK, P], U8, name="w4_planes", align_bytes=64)
        for a in range(PASSES):
            vector_copy(
                out=w4_codes[:, a].rearrange("p u (g b) -> p u g b", b=2),
                in_=w4_rows[:, a].rearrange("p (g u b) -> p u g b", u=PACK, b=2),
            )

        c_mx = [[mx_tiles("c%d%d" % (a, h), BANK) for h in range(HALVES)] for a in range(PASSES)]
        wk_mx = [mx_tiles("wk%d" % a, D) for a in range(PASSES)]
        kc_mx = mx_tiles("kc", J)
        kc_f32 = keep.tile([P, PACK, J], F32, name="kc_f32")
        kc_banks = {}
        whole = slice(0, BANK)

        def kc_pass(a, h):
            codes, scales = wk_mx[a]
            for u in range(PACK):
                if a == 0:
                    kc_banks[h, u] = bank(PACK * h + u, "kc_bank%d%d" % (h, u))
                matmul(kc_banks[h, u][:], codes[:, span(u, P)].bitcast(FP8X4), scales[:, span(u, P)], c_mx[a][h], whole, a == 0, a == PASSES - 1)

        def kc_out(h):
            for u in range(PACK):
                scalar_copy(out=kc_f32[:, u, span(h, BANK)], in_=kc_banks[h, u][:])

        c00, c01 = staged("c00"), staged("c01")
        interleave(vector_copy, c00[:], c0_rows[:, :, span(0, BANK)], 0, BANK)
        interleave(scalar_copy, c01[:], c0_rows[:, :, span(1, BANK)], 0, BANK)
        vector_copy(out=w4_planes[:], in_=w4_scale_rows[:].rearrange("p a (g u) -> p a u g", u=PACK))
        quantize(c00[:], c_mx[0][0], whole)
        wk0 = staged("wk0")
        interleave_dealt(scalar_copy, wk0[:], wk_rows[0][:])

        kb_rows = keep.tile([P, J], F32, name="kb_rows")
        for s in range(2):
            spread = bank(6 + s, "kb_bank%d" % s)
            for e in range(4):
                nc.tensor.transpose(spread[:, span(e, P)], kb_cols[:, span(4 * s + e, 1)].to_broadcast([P, P]), ident[:])
            scalar_copy(
                out=kb_rows[:].rearrange("p (n e) -> p n e", e=J // P)[:, :, span(s, 4)],
                in_=spread[:].rearrange("p (e n) -> p n e", e=4),
            )

        quantize(c01[:], c_mx[0][1], whole)
        wk1 = staged("wk1")
        interleave_dealt(vector_copy, wk1[:], wk_rows[1][:])
        quantize(wk0[:], wk_mx[0], whole)
        kc_pass(0, 0)
        quantize(wk1[:], wk_mx[1], whole)
        c10 = staged("c10")
        interleave(vector_copy, c10[:], c1_rows[0][:], 0, C_VECTOR)
        interleave(scalar_copy, c10[:], c1_rows[0][:], C_VECTOR, BANK)
        quantize(c10[:], c_mx[1][0], whole)
        kc_pass(1, 0)
        kc_pass(0, 1)
        kc_out(0)
        c11 = staged("c11")
        interleave(vector_copy, c11[:], c1_rows[1][:], 0, BANK)
        quantize(c11[:], c_mx[1][1], whole)
        kc_pass(1, 1)

        x_staged = [keep.tile([P, PASSES * K_PASS], BF16, name="x_staged%d" % i, align_bytes=64) for i in range(TILES)]
        x_mx = [mx_tiles("x%d" % i, PASSES * P) for i in range(TILES)]
        qr_staged = [keep.tile([P, K_PASS], BF16, name="qr_staged%d" % i, align_bytes=64) for i in range(TILES)]
        qr_mx = [mx_tiles("qr%d" % i, P) for i in range(TILES)]
        scores = [keep.tile([P, J], F32, name="scores%d" % i) for i in range(TILES)]
        qr_banks = {}
        sc_banks = {}

        def x_round(i, a):
            if i < EARLY_TILES:
                rows = x_early[a][:, :, span(i, P)]
            else:
                rows = x_late[a][:, :, span(i - EARLY_TILES, P)]
            interleave(vector_copy if i < VECTOR_TILES else scalar_copy, x_staged[i][:, span(a, K_PASS)], rows, 0, P)

        def qr_pass(i, a):
            if a == 0:
                qr_banks[i] = bank(i % 4, "qr_bank%d" % i)
            for u in range(PACK):
                matmul(
                    qr_banks[i][:, span(u, P)], w4_codes[:, a, u, :].bitcast(FP4X4), w4_planes[:, a, u, :], x_mx[i], span(a, P),
                    a == 0 and u == 0, a == PASSES - 1 and u == PACK - 1,
                )

        def qr_one_pass(i, a):
            quantize(x_staged[i][:, span(a, K_PASS)], x_mx[i], span(a, P))
            qr_pass(i, a)

        def qr_both_passes(i):
            quantize(x_staged[i][:], x_mx[i], slice(0, PASSES * P))
            for a in range(PASSES):
                qr_pass(i, a)

        def qr_out(i):
            scalar_copy(
                out=qr_staged[i][:].rearrange("p (m t) -> p m t", t=PACK),
                in_=qr_banks[i][:].rearrange("p (t m) -> p m t", t=PACK),
            )

        def qr_quantize(i):
            quantize(qr_staged[i][:], qr_mx[i], slice(0, P))

        def sc_matmul(i):
            codes, scales = qr_mx[i]
            for h in range(HALVES):
                sc_banks[i, h] = bank(4 + 2 * (i % 2) + h, "sc_bank%d%d" % (i, h))
                matmul(sc_banks[i, h][:], codes[:].bitcast(FP8X4), scales[:], kc_mx, span(h, BANK), True, True)

        def sc_out(i, h):
            cols = span(h, BANK)
            nc.vector.scalar_tensor_tensor(
                out=scores[i][:, cols], in0=sc_banks[i, h][:], scalar=SCORE_SCALE, in1=kb_rows[:, cols], op0=ALU.mult, op1=ALU.add
            )
            if i >= HALF_STORES_FROM:
                nc.sync.dma_start(out=out_0[span(i, P), cols], in_=scores[i][:, cols])
            elif h == HALVES - 1:
                nc.sync.dma_start(out=out_0[span(i, P), :], in_=scores[i][:])

        kc0, kc1 = staged("kc0"), staged("kc1")
        for i in range(BY_PASS_TILES):
            x_round(i, 0)
        interleave(vector_copy, kc0[:], kc_f32[:, :, span(0, BANK)], 0, BANK)
        kc_out(1)
        nc.sync.dma_start(out=out_1.rearrange("(p t) j -> p t j", t=PACK), in_=kc_f32[:])
        qr_one_pass(0, 0)
        qr_one_pass(1, 0)
        quantize(kc0[:], kc_mx, span(0, BANK))
        for i in range(BY_PASS_TILES):
            x_round(i, 1)
        for a in range(PASSES):
            x_round(BY_PASS_TILES, a)
        qr_one_pass(2, 0)
        qr_one_pass(0, 1)
        qr_one_pass(1, 1)
        interleave(vector_copy, kc1[:], kc_f32[:, :, span(1, BANK)], 0, BANK)
        qr_out(0)
        qr_one_pass(2, 1)
        qr_quantize(0)
        quantize(kc1[:], kc_mx, span(1, BANK))
        sc_matmul(0)
        qr_out(1)
        nc.sync.dma_start(out=out_2[0].rearrange("p j i -> p (j i)").bitcast(I32), in_=kc_mx[0][:].bitcast(I32))
        for q in range(P // QUADRANT):
            nc.sync.dma_start(out=out_3[0, span(q, 4), :].bitcast(I32), in_=kc_mx[1][QUADRANT * q : QUADRANT * q + 4, :].bitcast(I32))
        x_round(4, 0)
        for i in range(TILES):
            if i + 1 < TILES:
                qr_quantize(i + 1)
                sc_matmul(i + 1)
            if i + 2 < TILES:
                qr_out(i + 2)
            if i + 4 < TILES:
                x_round(i + 4, 1)
            if i + 5 < TILES:
                x_round(i + 5, 0)
            sc_out(i, 0)
            if i + 3 < TILES:
                qr_both_passes(i + 3)
            sc_out(i, 1)
